import numpy as np, ml_dtypes
CORES = [51,54,179,182]
N = 4
S, B = 2, 512
def setup_inputs(rng):
    a = (rng.standard_normal((128, 128), dtype=np.float32) / 12).astype(ml_dtypes.bfloat16)
    return {"x": rng.standard_normal((N, 128, S * B), dtype=np.float32).astype(ml_dtypes.bfloat16), "a": np.broadcast_to(a, (N, 128, 128)).copy(), "at": np.broadcast_to(a.T, (N, 128, 128)).copy()}
def setup_inputs_big(rng):
    d = setup_inputs(rng)
    for k in ("x",): d[k] = (d[k].astype(np.float32) * 1048576.0).astype(d[k].dtype)
    return d
def setup_inputs_small(rng):
    d = setup_inputs(rng)
    for k in ("x",): d[k] = (d[k].astype(np.float32) * (1 / 1048576.0)).astype(d[k].dtype)
    return d
def setup_inputs_apart(rng):
    d = setup_inputs(rng)
    f = (10.0 ** rng.permutation(np.linspace(-1.5, 1.5, N))).astype(np.float32).reshape(N, 1, 1)
    for k in ("x",): d[k] = (d[k].astype(np.float32) * f).astype(d[k].dtype)
    return d
def reference(x, a, at):
    X, A = x.astype(np.float64), a.astype(np.float64)
    y = np.zeros((N, 128, S * B)); h = np.zeros((128, B))
    for r in range(N):
        for s in range(S):
            h = A[r].T @ h + X[r][:, B * s:B * s + B]
            y[r][:, B * s:B * s + B] = h
    return {"y": y.astype(ml_dtypes.bfloat16)}

@@ -1,0 +1,184 @@
+from concourse.bass import DstId, RemoteDMATransfer
+from concourse.mybir import AluOpType
+
+P, B = 128, 512
+
+SCRATCH = {
+    "x0s": ("sbuf", [P, B], "bfloat16"),
+    "x1s": ("sbuf", [P, B], "bfloat16"),
+    "ats": ("sbuf", [P, P], "bfloat16"),
+    "pw": ("sbuf", [P, 7 * P], "bfloat16"),
+    "l1": ("sbuf", [P, B], "bfloat16"),
+    "land0": ("sbuf", [P, B], "bfloat16"),
+    "land1": ("sbuf", [P, B], "bfloat16"),
+    "land2": ("sbuf", [P, B], "bfloat16"),
+    "y0s": ("sbuf", [P, B], "bfloat16"),
+    "y1s": ("sbuf", [P, B], "bfloat16"),
+    "pl": ("psum", [P, B], "float32"),
+    "p0": ("psum", [P, B], "float32"),
+    "p1": ("psum", [P, B], "float32"),
+    "w1": ("psum", [P, B], "float32"),
+    "w2": ("psum", [P, B], "float32"),
+    "w3": ("psum", [P, B], "float32"),
+}
+SEMAPHORES = ["ld_x0", "ld_x1", "ld_a", "ld_at", "m_l1", "v_l1", "m_w", "v_w", "m_y0", "m_y1", "v_y0", "v_y1",
+              "arr0", "arr1", "arr2", "sent", "st0", "st1"]
+
+
+def _engines(mask):
+    return [1 << i for i in range(mask.bit_length()) if (mask >> i) & 1]
+
+
+def _join(bits):
+    m = 0
+    for b in bits:
+        m |= b
+    return m
+
+
+def _same_chip(topo, a, b):
+    return topo.host(a) == topo.host(b) and topo.chip(a) == topo.chip(b)
+
+
+def _plan(topo, cores, q):
+    src = cores[q]
+    later = cores[q + 1:]
+    far = [d for d in later if not _same_chip(topo, src, d)]
+    near = [d for d in later if _same_chip(topo, src, d)]
+    used, out_far, out_near = [], [], []
+    for i, d in enumerate(far):
+        e = _engines(topo.mask(src, d))
+        n = len(e) // len(far)
+        part = e[i * n:(i + 1) * n]
+        used += part
+        out_far.append((d, _join(part)))
+    for d in near:
+        e = [b for b in _engines(topo.mask(src, d)) if b not in used]
+        part = e[:8]
+        used += part
+        out_near.append((d, _join(part)))
+    return out_far, out_near
+
+
+def _col(k):
+    return (k - 1) * P if k <= 2 else k * P
+
+
+def rank_program(g, core, T, topo):
+    r = T.rank_of(core)
+    if r is None:
+        return
+    cores = list(T.cores)
+    sem = T.sem
+    te, ve, sy, sc = g.tensor, g.vector, g.sync, g.scalar
+    far, near = _plan(topo, cores, r)
+    sends = bool(far or near)
+
+    def power(k):
+        return T.pw[:, _col(k):_col(k) + P]
+
+    a = power(1)
+    at2 = T.pw[:, 2 * P:3 * P]
+
+    sy.dma_start(T.x0s[:], T.x[:, 0:B]).then_inc(sem.ld_x0, 16)
+    sc.dma_start(a, T.a[:, :]).then_inc(sem.ld_a, 16)
+    sc.dma_start(T.x1s[:], T.x[:, B:2 * B]).then_inc(sem.ld_x1, 16)
+    if r > 0:
+        sy.dma_start(T.ats[:], T.at[:, :]).then_inc(sem.ld_at, 16)
+
+    te.wait_ge(sem.ld_a, 16)
+    te.wait_ge(sem.ld_x0, 16)
+    ve.wait_ge(sem.ld_x1, 16)
+    if sends:
+        te.matmul(T.pl[:], a, T.x0s[:], True, True).then_inc(sem.m_l1, 1)
+        ve.wait_ge(sem.m_l1, 1)
+        ve.tensor_tensor(T.l1[:], T.pl[:], T.x1s[:], AluOpType.add).then_inc(sem.v_l1, 1)
+        g.wait_ge(sem.v_l1, 1)
+        land = T["land%d" % r]
+        arr = sem["arr%d" % r]
+        total = 0
+        if far:
+            trs = []
+            for d, m in far:
+                rid, pid = topo.addr(d, core)
+                trs.append(RemoteDMATransfer(dst_ids=[DstId(rid=rid, pnc=pid)], dma_engine_mask=m, remote_sem=arr,
+                                             src=T.l1[:], dst=land[:]))
+                total += len(_engines(m))
+            g.remote_dma_fused(trs, local_sem=sem.sent)
+        for d, m in near:
+            rid, pid = topo.addr(d, core)
+            g.remote_dma(land[:], T.l1[:], arr, sem.sent, pid, rid, m)
+            total += len(_engines(m))
+        g.wait_ge(sem.sent, total)
+
+    if r == 0:
+        sy.wait_ge(sem.ld_x0, 16)
+        sy.dma_start(T.y[:, 0:B], T.x0s[:]).then_inc(sem.st0, 16)
+        sc.wait_ge(sem.v_l1, 1)
+        sc.dma_start(T.y[:, B:2 * B], T.l1[:]).then_inc(sem.st1, 16)
+        sy.wait_ge(sem.st0, 16)
+        sc.wait_ge(sem.st1, 16)
+        return
+
+    te.matmul(T.p1[:], a, T.x0s[:], True, False)
+
+    te.wait_ge(sem.ld_at, 16)
+    n1 = 1 if r == 1 else 2
+    te.matmul(T.w1[:, 0:P], T.ats[:], a, True, True).then_inc(sem.m_w, 1)
+    if n1 == 2:
+        te.matmul(T.w1[:, P:2 * P], a, T.ats[:], True, True).then_inc(sem.m_w, 1)
+    ve.wait_ge(sem.m_w, n1)
+    ve.tensor_copy(T.pw[:, P:P + n1 * P], T.w1[:, 0:n1 * P]).then_inc(sem.v_w, 1)
+    nm, nv = n1, 1
+    for lev in range(2, r + 1):
+        w = T["w%d" % lev]
+        src, dst = _col(2 * lev - 3), _col(2 * lev - 1)
+        te.wait_ge(sem.v_w, nv)
+        te.matmul(w[:, 0:2 * P], at2, T.pw[:, src:src + 2 * P], True, True).then_inc(sem.m_w, 1)
+        nm += 1
+        ve.wait_ge(sem.m_w, nm)
+        ve.tensor_copy(T.pw[:, dst:dst + 2 * P], w[:, 0:2 * P]).then_inc(sem.v_w, 1)
+        nv += 1
+    te.wait_ge(sem.v_w, nv)
+
+    def count(q):
+        f, n = _plan(topo, cores, q)
+        return [len(_engines(m)) for d, m in f + n if d == core][0]
+
+    early = [q for q in range(r) if _same_chip(topo, cores[q], core)]
+    late = [q for q in range(r) if q not in early]
+    if not late:
+        early, late = [], early
+    opened = [False]
+
+    def add0(q, stop):
+        i = te.matmul(T.p0[:], power(2 * (r - 1 - q) + 1), T["land%d" % q][:], not opened[0], stop)
+        opened[0] = True
+        return i
+
+    def add1(q, stop):
+        return te.matmul(T.p1[:], power(2 * (r - 1 - q) + 2), T["land%d" % q][:], False, stop)
+
+    for q in early:
+        te.wait_ge(sem["arr%d" % q], count(q))
+        add0(q, False)
+        add1(q, False)
+    for q in late:
+        te.wait_ge(sem["arr%d" % q], count(q))
+        i = add0(q, q == late[-1])
+    i.then_inc(sem.m_y0, 1)
+    for q in late:
+        i = add1(q, q == late[-1])
+    i.then_inc(sem.m_y1, 1)
+
+    ve.wait_ge(sem.ld_x0, 16)
+    ve.wait_ge(sem.m_y0, 1)
+    ve.tensor_tensor(T.y0s[:], T.p0[:], T.x0s[:], AluOpType.add).then_inc(sem.v_y0, 1)
+    ve.wait_ge(sem.m_y1, 1)
+    ve.tensor_tensor(T.y1s[:], T.p1[:], T.x1s[:], AluOpType.add).then_inc(sem.v_y1, 1)
+    sy.wait_ge(sem.v_y0, 1)
+    sy.dma_start(T.y[:, 0:B], T.y0s[:]).then_inc(sem.st0, 16)
+    sc.wait_ge(sem.v_y1, 1)
+    sc.dma_start(T.y[:, B:2 * B], T.y1s[:]).then_inc(sem.st1, 16)
+    sy.wait_ge(sem.st0, 16)
+    sc.wait_ge(sem.st1, 16)

@@ -2,6 +2,9 @@ from concourse.bass import DstId, RemoteDMATransfer
 from concourse.mybir import AluOpType
 
 P, B = 128, 512
+C = 2
+W = B // C
+NEAR = 4
 
 SCRATCH = {
     "x0s": ("sbuf", [P, B], "bfloat16"),
@@ -14,15 +17,13 @@ SCRATCH = {
     "land2": ("sbuf", [P, B], "bfloat16"),
     "y0s": ("sbuf", [P, B], "bfloat16"),
     "y1s": ("sbuf", [P, B], "bfloat16"),
-    "pl": ("psum", [P, B], "float32"),
-    "p0": ("psum", [P, B], "float32"),
-    "p1": ("psum", [P, B], "float32"),
-    "w1": ("psum", [P, B], "float32"),
-    "w2": ("psum", [P, B], "float32"),
-    "w3": ("psum", [P, B], "float32"),
+    "w": ("psum", [P, B], "float32"),
 }
-SEMAPHORES = ["ld_x0", "ld_x1", "ld_a", "ld_at", "m_l1", "v_l1", "m_w", "v_w", "m_y0", "m_y1", "v_y0", "v_y1",
-              "arr0", "arr1", "arr2", "sent", "st0", "st1"]
+SEMAPHORES = ["ld_x0", "ld_x1", "ld_a", "ld_at", "m_w", "v_w", "sent", "st0", "st1"]
+for _c in range(C):
+    for _n in ("pl", "p0", "p1"):
+        SCRATCH["%s_%d" % (_n, _c)] = ("psum", [P, B], "float32")
+    SEMAPHORES += ["%s_%d" % (_n, _c) for _n in ("m_l", "v_l", "m_y0", "m_y1", "v_y0", "v_y1", "arr0", "arr1", "arr2")]
 
 
 def _engines(mask):
@@ -44,20 +45,18 @@ def _plan(topo, cores, q):
     src = cores[q]
     later = cores[q + 1:]
     far = [d for d in later if not _same_chip(topo, src, d)]
-    near = [d for d in later if _same_chip(topo, src, d)]
-    used, out_far, out_near = [], [], []
-    for i, d in enumerate(far):
-        e = _engines(topo.mask(src, d))
-        n = len(e) // len(far)
-        part = e[i * n:(i + 1) * n]
-        used += part
-        out_far.append((d, _join(part)))
-    for d in near:
-        e = [b for b in _engines(topo.mask(src, d)) if b not in used]
-        part = e[:8]
-        used += part
-        out_near.append((d, _join(part)))
-    return out_far, out_near
+    far = [d for d in far if topo.die(d) == topo.die(src)] + [d for d in far if topo.die(d) != topo.die(src)]
+    far_mask = 0
+    for d in far:
+        far_mask = topo.mask(src, d) if far_mask == 0 else far_mask & topo.mask(src, d)
+    used = _engines(far_mask)
+    near = []
+    for d in later:
+        if _same_chip(topo, src, d):
+            part = [b for b in _engines(topo.mask(src, d)) if b not in used][:NEAR]
+            used = used + part
+            near.append((d, _join(part)))
+    return far, far_mask, near
 
 
 def _col(k):
@@ -71,11 +70,20 @@ def rank_program(g, core, T, topo):
     cores = list(T.cores)
     sem = T.sem
     te, ve, sy, sc = g.tensor, g.vector, g.sync, g.scalar
-    far, near = _plan(topo, cores, r)
+    far, far_mask, near = _plan(topo, cores, r)
     sends = bool(far or near)
 
     def power(k):
         return T.pw[:, _col(k):_col(k) + P]
+
+    def blk(t, c):
+        return t[:, c * W:(c + 1) * W]
+
+    def bank(name, c):
+        return T["%s_%d" % (name, c)][:, 0:W]
+
+    def s(name, c):
+        return sem["%s_%d" % (name, c)]
 
     a = power(1)
     at2 = T.pw[:, 2 * P:3 * P]
@@ -90,95 +98,85 @@ def rank_program(g, core, T, topo):
     te.wait_ge(sem.ld_x0, 16)
     ve.wait_ge(sem.ld_x1, 16)
     if sends:
-        te.matmul(T.pl[:], a, T.x0s[:], True, True).then_inc(sem.m_l1, 1)
-        ve.wait_ge(sem.m_l1, 1)
-        ve.tensor_tensor(T.l1[:], T.pl[:], T.x1s[:], AluOpType.add).then_inc(sem.v_l1, 1)
-        g.wait_ge(sem.v_l1, 1)
         land = T["land%d" % r]
-        arr = sem["arr%d" % r]
         total = 0
-        if far:
+        for c in range(C):
+            te.matmul(bank("pl", c), a, blk(T.x0s, c), True, True).then_inc(s("m_l", c), 1)
+            ve.wait_ge(s("m_l", c), 1)
+            ve.tensor_tensor(blk(T.l1, c), bank("pl", c), blk(T.x1s, c), AluOpType.add).then_inc(s("v_l", c), 1)
+            g.wait_ge(s("v_l", c), 1)
+            arr = s("arr%d" % r, c)
             trs = []
-            for d, m in far:
+            if far:
+                ids = [DstId(rid=topo.addr(d, core)[0], pnc=topo.addr(d, core)[1]) for d in far]
+                trs.append(RemoteDMATransfer(dst_ids=ids, dma_engine_mask=far_mask, remote_sem=arr,
+                                             srcs=[blk(T.l1, c)], dsts=[blk(land, c) for d in far]))
+                total += len(_engines(far_mask))
+            for d, m in near:
                 rid, pid = topo.addr(d, core)
                 trs.append(RemoteDMATransfer(dst_ids=[DstId(rid=rid, pnc=pid)], dma_engine_mask=m, remote_sem=arr,
-                                             src=T.l1[:], dst=land[:]))
+                                             srcs=[blk(T.l1, c)], dsts=[blk(land, c)]))
                 total += len(_engines(m))
             g.remote_dma_fused(trs, local_sem=sem.sent)
-        for d, m in near:
-            rid, pid = topo.addr(d, core)
-            g.remote_dma(land[:], T.l1[:], arr, sem.sent, pid, rid, m)
-            total += len(_engines(m))
         g.wait_ge(sem.sent, total)
 
     if r == 0:
         sy.wait_ge(sem.ld_x0, 16)
         sy.dma_start(T.y[:, 0:B], T.x0s[:]).then_inc(sem.st0, 16)
-        sc.wait_ge(sem.v_l1, 1)
+        for c in range(C):
+            sc.wait_ge(s("v_l", c), 1)
         sc.dma_start(T.y[:, B:2 * B], T.l1[:]).then_inc(sem.st1, 16)
         sy.wait_ge(sem.st0, 16)
         sc.wait_ge(sem.st1, 16)
         return
 
-    te.matmul(T.p1[:], a, T.x0s[:], True, False)
+    for c in range(C):
+        te.matmul(bank("p1", c), a, blk(T.x0s, c), True, False)
 
     te.wait_ge(sem.ld_at, 16)
     n1 = 1 if r == 1 else 2
-    te.matmul(T.w1[:, 0:P], T.ats[:], a, True, True).then_inc(sem.m_w, 1)
+    te.matmul(T.w[:, 0:P], T.ats[:], a, True, True).then_inc(sem.m_w, 1)
     if n1 == 2:
-        te.matmul(T.w1[:, P:2 * P], a, T.ats[:], True, True).then_inc(sem.m_w, 1)
+        te.matmul(T.w[:, P:2 * P], a, T.ats[:], True, True).then_inc(sem.m_w, 1)
     ve.wait_ge(sem.m_w, n1)
-    ve.tensor_copy(T.pw[:, P:P + n1 * P], T.w1[:, 0:n1 * P]).then_inc(sem.v_w, 1)
+    ve.tensor_copy(T.pw[:, P:P + n1 * P], T.w[:, 0:n1 * P]).then_inc(sem.v_w, 1)
     nm, nv = n1, 1
     for lev in range(2, r + 1):
-        w = T["w%d" % lev]
         src, dst = _col(2 * lev - 3), _col(2 * lev - 1)
         te.wait_ge(sem.v_w, nv)
-        te.matmul(w[:, 0:2 * P], at2, T.pw[:, src:src + 2 * P], True, True).then_inc(sem.m_w, 1)
+        te.matmul(T.w[:, 0:2 * P], at2, T.pw[:, src:src + 2 * P], True, True).then_inc(sem.m_w, 1)
         nm += 1
         ve.wait_ge(sem.m_w, nm)
-        ve.tensor_copy(T.pw[:, dst:dst + 2 * P], w[:, 0:2 * P]).then_inc(sem.v_w, 1)
+        ve.tensor_copy(T.pw[:, dst:dst + 2 * P], T.w[:, 0:2 * P]).then_inc(sem.v_w, 1)
         nv += 1
     te.wait_ge(sem.v_w, nv)
 
-    def count(q):
-        f, n = _plan(topo, cores, q)
-        return [len(_engines(m)) for d, m in f + n if d == core][0]
-
-    early = [q for q in range(r) if _same_chip(topo, cores[q], core)]
-    late = [q for q in range(r) if q not in early]
-    if not late:
-        early, late = [], early
-    opened = [False]
-
-    def add0(q, stop):
-        i = te.matmul(T.p0[:], power(2 * (r - 1 - q) + 1), T["land%d" % q][:], not opened[0], stop)
-        opened[0] = True
-        return i
-
-    def add1(q, stop):
-        return te.matmul(T.p1[:], power(2 * (r - 1 - q) + 2), T["land%d" % q][:], False, stop)
-
-    for q in early:
-        te.wait_ge(sem["arr%d" % q], count(q))
-        add0(q, False)
-        add1(q, False)
-    for q in late:
-        te.wait_ge(sem["arr%d" % q], count(q))
-        i = add0(q, q == late[-1])
-    i.then_inc(sem.m_y0, 1)
-    for q in late:
-        i = add1(q, q == late[-1])
-    i.then_inc(sem.m_y1, 1)
+    order = []
+    for q in range(r):
+        f, fm, n = _plan(topo, cores, q)
+        if core in f:
+            order.append((1 + f.index(core), q, len(_engines(fm))))
+        else:
+            order.append((0, q, [len(_engines(m)) for d, m in n if d == core][0]))
+    order.sort()
 
     ve.wait_ge(sem.ld_x0, 16)
-    ve.wait_ge(sem.m_y0, 1)
-    ve.tensor_tensor(T.y0s[:], T.p0[:], T.x0s[:], AluOpType.add).then_inc(sem.v_y0, 1)
-    ve.wait_ge(sem.m_y1, 1)
-    ve.tensor_tensor(T.y1s[:], T.p1[:], T.x1s[:], AluOpType.add).then_inc(sem.v_y1, 1)
-    sy.wait_ge(sem.v_y0, 1)
-    sy.dma_start(T.y[:, 0:B], T.y0s[:]).then_inc(sem.st0, 16)
-    sc.wait_ge(sem.v_y1, 1)
-    sc.dma_start(T.y[:, B:2 * B], T.y1s[:]).then_inc(sem.st1, 16)
-    sy.wait_ge(sem.st0, 16)
-    sc.wait_ge(sem.st1, 16)
+    for c in range(C):
+        for j, (place, q, n) in enumerate(order):
+            last = j == len(order) - 1
+            te.wait_ge(s("arr%d" % q, c), n)
+            k = 2 * (r - 1 - q) + 1
+            i0 = te.matmul(bank("p0", c), power(k), blk(T["land%d" % q], c), j == 0, last)
+            i1 = te.matmul(bank("p1", c), power(k + 1), blk(T["land%d" % q], c), False, last)
+        i0.then_inc(s("m_y0", c), 1)
+        i1.then_inc(s("m_y1", c), 1)
+        ve.wait_ge(s("m_y0", c), 1)
+        ve.tensor_tensor(blk(T.y0s, c), bank("p0", c), blk(T.x0s, c), AluOpType.add).then_inc(s("v_y0", c), 1)
+        ve.wait_ge(s("m_y1", c), 1)
+        ve.tensor_tensor(blk(T.y1s, c), bank("p1", c), blk(T.x1s, c), AluOpType.add).then_inc(s("v_y1", c), 1)
+        sy.wait_ge(s("v_y0", c), 1)
+        sy.dma_start(T.y[:, c * W:(c + 1) * W], blk(T.y0s, c)).then_inc(sem.st0, 16)
+        sc.wait_ge(s("v_y1", c), 1)
+        sc.dma_start(T.y[:, B + c * W:B + (c + 1) * W], blk(T.y1s, c)).then_inc(sem.st1, 16)
+    sy.wait_ge(sem.st0, 16 * C)
+    sc.wait_ge(sem.st1, 16 * C)

@@ -2,8 +2,9 @@ from concourse.bass import DstId, RemoteDMATransfer
 from concourse.mybir import AluOpType
 
 P, B = 128, 512
-C = 2
-W = B // C
+BLK = [(0, 128), (128, 352), (352, 512)]
+LDG = [(0, 128), (128, 512)]
+C = len(BLK)
 NEAR = 4
 
 SCRATCH = {
@@ -19,11 +20,14 @@ SCRATCH = {
     "y1s": ("sbuf", [P, B], "bfloat16"),
     "w": ("psum", [P, B], "float32"),
 }
-SEMAPHORES = ["ld_x0", "ld_x1", "ld_a", "ld_at", "m_w", "v_w", "sent", "st0", "st1"]
+SEMAPHORES = ["ld_a", "ld_at", "m_w", "v_w", "st0", "st1"]
+for _c in range(len(LDG)):
+    SEMAPHORES += ["ld_x0_%d" % _c, "ld_x1_%d" % _c]
 for _c in range(C):
-    for _n in ("pl", "p0", "p1"):
+    for _n in ("pa", "p1"):
         SCRATCH["%s_%d" % (_n, _c)] = ("psum", [P, B], "float32")
-    SEMAPHORES += ["%s_%d" % (_n, _c) for _n in ("m_l", "v_l", "m_y0", "m_y1", "v_y0", "v_y1", "arr0", "arr1", "arr2")]
+    SEMAPHORES += ["%s_%d" % (_n, _c) for _n in ("m_l", "v_l", "sent", "m_y0", "m_y1", "v_y0", "v_y1",
+                                                 "arr0", "arr1", "arr2")]
 
 
 def _engines(mask):
@@ -46,17 +50,19 @@ def _plan(topo, cores, q):
     later = cores[q + 1:]
     far = [d for d in later if not _same_chip(topo, src, d)]
     far = [d for d in far if topo.die(d) == topo.die(src)] + [d for d in far if topo.die(d) != topo.die(src)]
-    far_mask = 0
-    for d in far:
-        far_mask = topo.mask(src, d) if far_mask == 0 else far_mask & topo.mask(src, d)
-    used = _engines(far_mask)
-    near = []
-    for d in later:
-        if _same_chip(topo, src, d):
-            part = [b for b in _engines(topo.mask(src, d)) if b not in used][:NEAR]
-            used = used + part
-            near.append((d, _join(part)))
-    return far, far_mask, near
+    near = [d for d in later if _same_chip(topo, src, d)]
+    out, used = [], []
+    if far:
+        m = topo.mask(src, far[0])
+        for d in far:
+            m &= topo.mask(src, d)
+        used = _engines(m)
+        out.append((m, far))
+    for d in near:
+        part = [b for b in _engines(topo.mask(src, d)) if b not in used][:NEAR]
+        used = used + part
+        out.append((_join(part), [d]))
+    return out
 
 
 def _col(k):
@@ -70,61 +76,71 @@ def rank_program(g, core, T, topo):
     cores = list(T.cores)
     sem = T.sem
     te, ve, sy, sc = g.tensor, g.vector, g.sync, g.scalar
-    far, far_mask, near = _plan(topo, cores, r)
-    sends = bool(far or near)
+    plan = _plan(topo, cores, r)
+    sends = bool(plan)
+    far = [d for m, ds in plan for d in ds if not _same_chip(topo, core, d)]
 
     def power(k):
         return T.pw[:, _col(k):_col(k) + P]
 
     def blk(t, c):
-        return t[:, c * W:(c + 1) * W]
+        return t[:, BLK[c][0]:BLK[c][1]]
 
     def bank(name, c):
-        return T["%s_%d" % (name, c)][:, 0:W]
+        return T["%s_%d" % (name, c)][:, 0:BLK[c][1] - BLK[c][0]]
 
     def s(name, c):
         return sem["%s_%d" % (name, c)]
 
+    def grp(c):
+        return [i for i, (lo, hi) in enumerate(LDG) if lo <= BLK[c][0] and BLK[c][1] <= hi][0]
+
     a = power(1)
     at2 = T.pw[:, 2 * P:3 * P]
 
-    sy.dma_start(T.x0s[:], T.x[:, 0:B]).then_inc(sem.ld_x0, 16)
+    def load_x(q, i):
+        lo, hi = LDG[i]
+        q.dma_start(T.x0s[:, lo:hi], T.x[:, lo:hi]).then_inc(s("ld_x0", i), 16)
+        q.dma_start(T.x1s[:, lo:hi], T.x[:, B + lo:B + hi]).then_inc(s("ld_x1", i), 16)
+
     sc.dma_start(a, T.a[:, :]).then_inc(sem.ld_a, 16)
-    sc.dma_start(T.x1s[:], T.x[:, B:2 * B]).then_inc(sem.ld_x1, 16)
-    if r > 0:
+    load_x(sy, 0)
+    if r > 0 and not far:
+        sc.dma_start(T.ats[:], T.at[:, :]).then_inc(sem.ld_at, 16)
+    load_x(sc, 1)
+    if r > 0 and far:
         sy.dma_start(T.ats[:], T.at[:, :]).then_inc(sem.ld_at, 16)
 
     te.wait_ge(sem.ld_a, 16)
-    te.wait_ge(sem.ld_x0, 16)
-    ve.wait_ge(sem.ld_x1, 16)
-    if sends:
+    left = sum(len(_engines(m)) for m, ds in plan)
+    for c in range(C):
+        te.wait_ge(s("ld_x0", grp(c)), 16)
+        ve.wait_ge(s("ld_x1", grp(c)), 16)
+        if not sends:
+            continue
+        te.matmul(bank("pa", c), a, blk(T.x0s, c), True, True).then_inc(s("m_l", c), 1)
+        ve.wait_ge(s("m_l", c), 1)
+        ve.tensor_tensor(blk(T.l1, c), bank("pa", c), blk(T.x1s, c), AluOpType.add).then_inc(s("v_l", c), 1)
+        g.wait_ge(s("v_l", c), 1)
         land = T["land%d" % r]
-        total = 0
+        trs = []
+        for m, ds in plan:
+            ids = [DstId(rid=topo.addr(d, core)[0], pnc=topo.addr(d, core)[1]) for d in ds]
+            trs.append(RemoteDMATransfer(dst_ids=ids, dma_engine_mask=m, remote_sem=s("arr%d" % r, c),
+                                         srcs=[blk(T.l1, c)], dsts=[blk(land, c) for d in ds]))
+        g.remote_dma_fused(trs, local_sem=s("sent", c))
+    if sends:
         for c in range(C):
-            te.matmul(bank("pl", c), a, blk(T.x0s, c), True, True).then_inc(s("m_l", c), 1)
-            ve.wait_ge(s("m_l", c), 1)
-            ve.tensor_tensor(blk(T.l1, c), bank("pl", c), blk(T.x1s, c), AluOpType.add).then_inc(s("v_l", c), 1)
-            g.wait_ge(s("v_l", c), 1)
-            arr = s("arr%d" % r, c)
-            trs = []
-            if far:
-                ids = [DstId(rid=topo.addr(d, core)[0], pnc=topo.addr(d, core)[1]) for d in far]
-                trs.append(RemoteDMATransfer(dst_ids=ids, dma_engine_mask=far_mask, remote_sem=arr,
-                                             srcs=[blk(T.l1, c)], dsts=[blk(land, c) for d in far]))
-                total += len(_engines(far_mask))
-            for d, m in near:
-                rid, pid = topo.addr(d, core)
-                trs.append(RemoteDMATransfer(dst_ids=[DstId(rid=rid, pnc=pid)], dma_engine_mask=m, remote_sem=arr,
-                                             srcs=[blk(T.l1, c)], dsts=[blk(land, c)]))
-                total += len(_engines(m))
-            g.remote_dma_fused(trs, local_sem=sem.sent)
-        g.wait_ge(sem.sent, total)
+            g.wait_ge(s("sent", c), left)
 
     if r == 0:
-        sy.wait_ge(sem.ld_x0, 16)
-        sy.dma_start(T.y[:, 0:B], T.x0s[:]).then_inc(sem.st0, 16)
+        for i in range(len(LDG)):
+            sy.wait_ge(s("ld_x0", i), 16)
         for c in range(C):
             sc.wait_ge(s("v_l", c), 1)
+        sy.wait_ge(s("sent", 0), left)
+        sy.dma_start(T.y[:, 0:B], T.x0s[:]).then_inc(sem.st0, 16)
+        sc.wait_ge(s("sent", C - 1), left)
         sc.dma_start(T.y[:, B:2 * B], T.l1[:]).then_inc(sem.st1, 16)
         sy.wait_ge(sem.st0, 16)
         sc.wait_ge(sem.st1, 16)
@@ -153,30 +169,31 @@ def rank_program(g, core, T, topo):
 
     order = []
     for q in range(r):
-        f, fm, n = _plan(topo, cores, q)
-        if core in f:
-            order.append((1 + f.index(core), q, len(_engines(fm))))
-        else:
-            order.append((0, q, [len(_engines(m)) for d, m in n if d == core][0]))
+        for m, ds in _plan(topo, cores, q):
+            if core in ds:
+                order.append((not _same_chip(topo, cores[q], core), ds.index(core), q, len(_engines(m))))
     order.sort()
 
-    ve.wait_ge(sem.ld_x0, 16)
     for c in range(C):
-        for j, (place, q, n) in enumerate(order):
+        if sends:
+            te.wait_ge(s("v_l", c), 1)
+        for j, (off, place, q, n) in enumerate(order):
             last = j == len(order) - 1
             te.wait_ge(s("arr%d" % q, c), n)
             k = 2 * (r - 1 - q) + 1
-            i0 = te.matmul(bank("p0", c), power(k), blk(T["land%d" % q], c), j == 0, last)
+            i0 = te.matmul(bank("pa", c), power(k), blk(T["land%d" % q], c), j == 0, last)
             i1 = te.matmul(bank("p1", c), power(k + 1), blk(T["land%d" % q], c), False, last)
         i0.then_inc(s("m_y0", c), 1)
         i1.then_inc(s("m_y1", c), 1)
+        lo, hi = BLK[c]
+        ve.wait_ge(s("ld_x0", grp(c)), 16)
         ve.wait_ge(s("m_y0", c), 1)
-        ve.tensor_tensor(blk(T.y0s, c), bank("p0", c), blk(T.x0s, c), AluOpType.add).then_inc(s("v_y0", c), 1)
+        ve.tensor_tensor(blk(T.y0s, c), bank("pa", c), blk(T.x0s, c), AluOpType.add).then_inc(s("v_y0", c), 1)
         ve.wait_ge(s("m_y1", c), 1)
         ve.tensor_tensor(blk(T.y1s, c), bank("p1", c), blk(T.x1s, c), AluOpType.add).then_inc(s("v_y1", c), 1)
         sy.wait_ge(s("v_y0", c), 1)
-        sy.dma_start(T.y[:, c * W:(c + 1) * W], blk(T.y0s, c)).then_inc(sem.st0, 16)
+        sy.dma_start(T.y[:, lo:hi], blk(T.y0s, c)).then_inc(sem.st0, 16)
         sc.wait_ge(s("v_y1", c), 1)
-        sc.dma_start(T.y[:, B + c * W:B + (c + 1) * W], blk(T.y1s, c)).then_inc(sem.st1, 16)
+        sc.dma_start(T.y[:, B + lo:B + hi], blk(T.y1s, c)).then_inc(sem.st1, 16)
     sy.wait_ge(sem.st0, 16 * C)
     sc.wait_ge(sem.st1, 16 * C)

from concourse.bass import DstId, RemoteDMATransfer
from concourse.mybir import AluOpType

P, B = 128, 512
BLK = [(0, 128), (128, 352), (352, 512)]
LDG = [(0, 128), (128, 512)]
C = len(BLK)
NEAR = 4

SCRATCH = {
    "x0s": ("sbuf", [P, B], "bfloat16"),
    "x1s": ("sbuf", [P, B], "bfloat16"),
    "ats": ("sbuf", [P, P], "bfloat16"),
    "pw": ("sbuf", [P, 7 * P], "bfloat16"),
    "l1": ("sbuf", [P, B], "bfloat16"),
    "land0": ("sbuf", [P, B], "bfloat16"),
    "land1": ("sbuf", [P, B], "bfloat16"),
    "land2": ("sbuf", [P, B], "bfloat16"),
    "y0s": ("sbuf", [P, B], "bfloat16"),
    "y1s": ("sbuf", [P, B], "bfloat16"),
    "w": ("psum", [P, B], "float32"),
}
SEMAPHORES = ["ld_a", "ld_at", "m_w", "v_w", "st0", "st1"]
for _c in range(len(LDG)):
    SEMAPHORES += ["ld_x0_%d" % _c, "ld_x1_%d" % _c]
for _c in range(C):
    for _n in ("pa", "p1"):
        SCRATCH["%s_%d" % (_n, _c)] = ("psum", [P, B], "float32")
    SEMAPHORES += ["%s_%d" % (_n, _c) for _n in ("m_l", "v_l", "sent", "m_y0", "m_y1", "v_y0", "v_y1",
                                                 "arr0", "arr1", "arr2")]


def _engines(mask):
    return [1 << i for i in range(mask.bit_length()) if (mask >> i) & 1]


def _join(bits):
    m = 0
    for b in bits:
        m |= b
    return m


def _same_chip(topo, a, b):
    return topo.host(a) == topo.host(b) and topo.chip(a) == topo.chip(b)


def _plan(topo, cores, q):
    src = cores[q]
    later = cores[q + 1:]
    far = [d for d in later if not _same_chip(topo, src, d)]
    far = [d for d in far if topo.die(d) == topo.die(src)] + [d for d in far if topo.die(d) != topo.die(src)]
    near = [d for d in later if _same_chip(topo, src, d)]
    out, used = [], []
    if far:
        m = topo.mask(src, far[0])
        for d in far:
            m &= topo.mask(src, d)
        used = _engines(m)
        out.append((m, far))
    for d in near:
        part = [b for b in _engines(topo.mask(src, d)) if b not in used][:NEAR]
        used = used + part
        out.append((_join(part), [d]))
    return out


def _col(k):
    return (k - 1) * P if k <= 2 else k * P


def rank_program(g, core, T, topo):
    r = T.rank_of(core)
    if r is None:
        return
    cores = list(T.cores)
    sem = T.sem
    te, ve, sy, sc = g.tensor, g.vector, g.sync, g.scalar
    plan = _plan(topo, cores, r)
    sends = bool(plan)
    far = [d for m, ds in plan for d in ds if not _same_chip(topo, core, d)]

    def power(k):
        return T.pw[:, _col(k):_col(k) + P]

    def blk(t, c):
        return t[:, BLK[c][0]:BLK[c][1]]

    def bank(name, c):
        return T["%s_%d" % (name, c)][:, 0:BLK[c][1] - BLK[c][0]]

    def s(name, c):
        return sem["%s_%d" % (name, c)]

    def grp(c):
        return [i for i, (lo, hi) in enumerate(LDG) if lo <= BLK[c][0] and BLK[c][1] <= hi][0]

    a = power(1)
    at2 = T.pw[:, 2 * P:3 * P]

    def load_x(q, i):
        lo, hi = LDG[i]
        q.dma_start(T.x0s[:, lo:hi], T.x[:, lo:hi]).then_inc(s("ld_x0", i), 16)
        q.dma_start(T.x1s[:, lo:hi], T.x[:, B + lo:B + hi]).then_inc(s("ld_x1", i), 16)

    sc.dma_start(a, T.a[:, :]).then_inc(sem.ld_a, 16)
    load_x(sy, 0)
    if r > 0 and not far:
        sc.dma_start(T.ats[:], T.at[:, :]).then_inc(sem.ld_at, 16)
    load_x(sc, 1)
    if r > 0 and far:
        sy.dma_start(T.ats[:], T.at[:, :]).then_inc(sem.ld_at, 16)

    te.wait_ge(sem.ld_a, 16)
    left = sum(len(_engines(m)) for m, ds in plan)
    for c in range(C):
        te.wait_ge(s("ld_x0", grp(c)), 16)
        ve.wait_ge(s("ld_x1", grp(c)), 16)
        if not sends:
            continue
        te.matmul(bank("pa", c), a, blk(T.x0s, c), True, True).then_inc(s("m_l", c), 1)
        ve.wait_ge(s("m_l", c), 1)
        ve.tensor_tensor(blk(T.l1, c), bank("pa", c), blk(T.x1s, c), AluOpType.add).then_inc(s("v_l", c), 1)
        g.wait_ge(s("v_l", c), 1)
        land = T["land%d" % r]
        trs = []
        for m, ds in plan:
            ids = [DstId(rid=topo.addr(d, core)[0], pnc=topo.addr(d, core)[1]) for d in ds]
            trs.append(RemoteDMATransfer(dst_ids=ids, dma_engine_mask=m, remote_sem=s("arr%d" % r, c),
                                         srcs=[blk(T.l1, c)], dsts=[blk(land, c) for d in ds]))
        g.remote_dma_fused(trs, local_sem=s("sent", c))
    if sends:
        for c in range(C):
            g.wait_ge(s("sent", c), left)

    if r == 0:
        for i in range(len(LDG)):
            sy.wait_ge(s("ld_x0", i), 16)
        for c in range(C):
            sc.wait_ge(s("v_l", c), 1)
        sy.wait_ge(s("sent", 0), left)
        sy.dma_start(T.y[:, 0:B], T.x0s[:]).then_inc(sem.st0, 16)
        sc.wait_ge(s("sent", C - 1), left)
        sc.dma_start(T.y[:, B:2 * B], T.l1[:]).then_inc(sem.st1, 16)
        sy.wait_ge(sem.st0, 16)
        sc.wait_ge(sem.st1, 16)
        return

    for c in range(C):
        te.matmul(bank("p1", c), a, blk(T.x0s, c), True, False)

    te.wait_ge(sem.ld_at, 16)
    n1 = 1 if r == 1 else 2
    te.matmul(T.w[:, 0:P], T.ats[:], a, True, True).then_inc(sem.m_w, 1)
    if n1 == 2:
        te.matmul(T.w[:, P:2 * P], a, T.ats[:], True, True).then_inc(sem.m_w, 1)
    ve.wait_ge(sem.m_w, n1)
    ve.tensor_copy(T.pw[:, P:P + n1 * P], T.w[:, 0:n1 * P]).then_inc(sem.v_w, 1)
    nm, nv = n1, 1
    for lev in range(2, r + 1):
        src, dst = _col(2 * lev - 3), _col(2 * lev - 1)
        te.wait_ge(sem.v_w, nv)
        te.matmul(T.w[:, 0:2 * P], at2, T.pw[:, src:src + 2 * P], True, True).then_inc(sem.m_w, 1)
        nm += 1
        ve.wait_ge(sem.m_w, nm)
        ve.tensor_copy(T.pw[:, dst:dst + 2 * P], T.w[:, 0:2 * P]).then_inc(sem.v_w, 1)
        nv += 1
    te.wait_ge(sem.v_w, nv)

    order = []
    for q in range(r):
        for m, ds in _plan(topo, cores, q):
            if core in ds:
                order.append((not _same_chip(topo, cores[q], core), ds.index(core), q, len(_engines(m))))
    order.sort()

    for c in range(C):
        if sends:
            te.wait_ge(s("v_l", c), 1)
        for j, (off, place, q, n) in enumerate(order):
            last = j == len(order) - 1
            te.wait_ge(s("arr%d" % q, c), n)
            k = 2 * (r - 1 - q) + 1
            i0 = te.matmul(bank("pa", c), power(k), blk(T["land%d" % q], c), j == 0, last)
            i1 = te.matmul(bank("p1", c), power(k + 1), blk(T["land%d" % q], c), False, last)
        i0.then_inc(s("m_y0", c), 1)
        i1.then_inc(s("m_y1", c), 1)
        lo, hi = BLK[c]
        ve.wait_ge(s("ld_x0", grp(c)), 16)
        ve.wait_ge(s("m_y0", c), 1)
        ve.tensor_tensor(blk(T.y0s, c), bank("pa", c), blk(T.x0s, c), AluOpType.add).then_inc(s("v_y0", c), 1)
        ve.wait_ge(s("m_y1", c), 1)
        ve.tensor_tensor(blk(T.y1s, c), bank("p1", c), blk(T.x1s, c), AluOpType.add).then_inc(s("v_y1", c), 1)
        sy.wait_ge(s("v_y0", c), 1)
        sy.dma_start(T.y[:, lo:hi], blk(T.y0s, c)).then_inc(sem.st0, 16)
        sc.wait_ge(s("v_y1", c), 1)
        sc.dma_start(T.y[:, B + lo:B + hi], blk(T.y1s, c)).then_inc(sem.st1, 16)
    sy.wait_ge(sem.st0, 16 * C)
    sc.wait_ge(sem.st1, 16 * C)
